import numpy as np
import ml_dtypes


def mxq(x, axis, fmt="e4m3"):
    dtype, down = {"e4m3": (ml_dtypes.float8_e4m3fn, 7), "e5m2": (ml_dtypes.float8_e5m2, 14)}[fmt]
    v = np.moveaxis(np.asarray(x, np.float32).astype(ml_dtypes.bfloat16).astype(np.float64), axis, -1)
    blocks = v.reshape(v.shape[:-1] + (-1, 32))
    amax = np.abs(blocks).max(-1, keepdims=True)
    byte = np.maximum(np.where(amax > 0, np.frexp(amax)[1] - 1 + 127, 0) - down, 1)
    scale = np.exp2(byte - 127.0)
    codes = (blocks / scale).astype(np.float32).astype(dtype).astype(np.float64)
    return np.moveaxis((codes * scale).reshape(v.shape), -1, axis)


WIDE = False


def mx_kscale(k):
    if not WIDE:
        return np.ones(k)
    levels = np.array([10, -10, 5, -5, 0])
    if k % 512:
        return np.exp2(np.random.permutation(np.resize(levels, k // 32))).repeat(32)
    a = np.empty((k // 512, 16))
    for p in range(k // 512):
        a[p, :8] = np.random.permutation(np.resize(levels, 8))
        for g in range(8):
            far = levels[np.abs(levels - a[p, g]) >= 10]
            a[p, g + 8] = far[np.random.randint(len(far))]
    return np.exp2(a.ravel()).repeat(32)


def f64(x):
    return np.asarray(x).astype(np.float64)


def striped(idx):
    return np.tile(np.asarray(idx).reshape(-1, 16).T, (8, 1)).astype(np.uint16)


def unstriped(offs):
    return offs[:16].T.reshape(-1).astype(np.int64)


E2M1 = np.array([0.0, 0.5, 1.0, 1.5, 2.0, 3.0, 4.0, 6.0, -0.0, -0.5, -1.0, -1.5, -2.0, -3.0, -4.0, -6.0])


def pack_weight(w, fmt):
    k, n = w.shape
    w = f64(np.asarray(w, np.float32).astype(ml_dtypes.bfloat16)).reshape(k // 32, 32, n)
    amax = np.abs(w).max(1)
    if fmt == "e4m3":
        byte = np.frexp(amax)[1] - 1 + 127 - 7
    else:
        mant, ex = np.frexp(amax / 6.0)
        byte = np.where(mant > 0.5, ex, ex - 1) + 127
    byte = np.clip(np.where(amax > 0, byte, 1), 1, 254)
    scaled = (w * np.exp2(127.0 - byte)[:, None, :]).reshape(k, n).astype(np.float32)
    by_word = np.ascontiguousarray(scaled.reshape(k // 512, 128, 4, n).transpose(0, 1, 3, 2))
    if fmt == "e4m3":
        words = by_word.astype(ml_dtypes.float8_e4m3fn).view(np.uint8)
    else:
        c = by_word.astype(ml_dtypes.float4_e2m1fn).view(np.uint8) & 0xF
        words = (c[..., 0::2] | (c[..., 1::2] << 4)).reshape(k // 512, 128, 2 * n)
    return np.ascontiguousarray(words), np.ascontiguousarray(byte.astype(np.uint8).reshape(k // 512, 16, n))


def unpack_weight(words, scales, fmt):
    g, _, n = scales.shape
    words = np.ascontiguousarray(words).reshape(g, 128, n, -1)
    if fmt == "e4m3":
        vals = words.view(ml_dtypes.float8_e4m3fn).astype(np.float64)
    else:
        nib = np.empty((g, 128, n, 4), np.uint8)
        nib[..., 0::2] = words & 0xF
        nib[..., 1::2] = words >> 4
        vals = E2M1[nib]
    vals = vals * np.repeat(np.exp2(scales.astype(np.float64) - 127.0), 8, axis=1)[..., None]
    return vals.transpose(0, 1, 3, 2).reshape(g * 512, n)


def bf(x):
    return np.asarray(x, np.float32).astype(ml_dtypes.bfloat16)


def planes(Y):
    r, m = Y.shape
    b = f64(bf(Y)).reshape(r // 32, 32, m)
    amax = np.abs(b).max(1)
    byte = np.clip(np.where(amax > 0, np.frexp(amax)[1] - 1 + 127 - 7, 1), 1, 254)
    codes = (b * np.exp2(127.0 - byte)[:, None, :]).reshape(r, m).astype(np.float32).astype(ml_dtypes.float8_e4m3fn).view(np.uint8)
    words = codes.reshape(r // 512, 128, 4, m).transpose(0, 1, 3, 2)
    return np.ascontiguousarray(words), np.ascontiguousarray(byte.astype(np.uint8).reshape(r // 512, 16, m))


D, E, T, I, Q, G = 512, 512, 2048, 512, 256, 32


def setup_inputs():
    n = np.random.standard_normal
    idx = np.random.permutation(T)[:I]
    fd = mx_kscale(D)
    fe = mx_kscale(E)
    fi = mx_kscale(I)
    ti = np.ones(T)
    ti[idx] = fi
    keysp = pack_weight(n((D, T)) / fd[:, None], "e2m1")
    valsp = pack_weight(n((E, T)) / fe[:, None], "e2m1")
    return {
        "query": (n((D, Q)) * 0.7 / np.sqrt(D) * fd[:, None]).astype(np.float32),
        "keys_words": keysp[0],
        "keys_scales": keysp[1],
        "reserve": (np.random.uniform(1.0, 8.0, (I, 1))).astype(np.float32),
        "us": (np.random.uniform(0.5, 2.0, (I, 1))).astype(np.float32),
        "gout": (n((E, Q)) * 1 / np.sqrt(E) * fe[:, None]).astype(np.float32),
        "vals_words": valsp[0],
        "vals_scales": valsp[1],
        "fs": (np.random.uniform(1.0, 4.0, (I, 1)) * fi[:, None]).astype(np.float32),
        "keyrows": (n((D, T)) / ti).astype(np.float32),
        "res": (n((D, Q)) * 1.0).astype(np.float32),
        "offs": striped(idx),
    }


def reference(query, keys_words, keys_scales, reserve, us, gout, vals_words, vals_scales, fs, keyrows, res, offs):
    idx = unstriped(offs)
    keysu = unpack_weight(keys_words, keys_scales, "e2m1")
    valsu = unpack_weight(vals_words, vals_scales, "e2m1")
    keysidxg = keysu[:, idx]
    queryq = mxq(f64(query), 0, "e4m3")
    a = keysidxg.T @ queryq
    p = np.exp(a)
    b = f64(us) / (p.reshape(I, G, Q // G).sum(axis=2) + f64(reserve))
    br = np.repeat(b, Q // G, axis=1)
    valsidxg = valsu[:, idx]
    goutq = mxq(f64(gout), 0, "e4m3")
    c0 = valsidxg.T @ goutq
    dbr = c0 * p
    db = dbr.reshape(I, G, Q // G).sum(axis=2)
    e1 = db * f64(us) / np.square(p.reshape(I, G, Q // G).sum(axis=2) + f64(reserve)) * (-1.0)
    r1 = np.repeat(e1, Q // G, axis=1)
    dp = c0 * br + r1
    da = dp * p
    gs = da * f64(fs)
    kt = f64(keyrows)[:, idx].T
    ktq = mxq(kt, 0, "e4m3")
    gsq = mxq(gs, 0, "e4m3")
    gq = ktq.T @ gsq
    y = gq + f64(res)
    words, scales = planes(y)
    return y, words, scales

@@ -1,0 +1,314 @@
+from contextlib import ExitStack
+
+import concourse.mybir as mybir
+from concourse.masks import make_identity
+
+D, E, T, I, Q, G = 512, 512, 2048, 512, 256, 32
+FLOPS = 2 * I * Q * (D + E + D)
+
+F32 = mybir.dt.float32
+BF16 = mybir.dt.bfloat16
+I32 = mybir.dt.int32
+U32 = mybir.dt.uint32
+U16 = mybir.dt.uint16
+U8 = mybir.dt.uint8
+FP8X4 = mybir.dt.float8_e4m3fn_x4
+FP4X4 = mybir.dt.float4_e2m1fn_x4
+ALU = mybir.AluOpType
+ACT = mybir.ActivationFunctionType
+
+P = 128
+PACK = 4
+TEAM = Q // G
+HALF = Q // 2
+GH = G // 2
+SCALAR_PLANE = 1
+
+
+def tile_attend_bteamshares_q_pl_kernel(
+    tc, query, keys_words, keys_scales, reserve, us, gout, vals_words, vals_scales, fs, keyrows, res, offs,
+    out_0, out_1, out_2,
+):
+    nc = tc.nc
+    with ExitStack() as ctx:
+        sb = ctx.enter_context(tc.tile_pool(name="sb", bufs=1))
+        ps = ctx.enter_context(tc.psum_pool(name="ps", bufs=1))
+
+        def sbuf(name, shape, dtype, tag=None):
+            return sb.tile(shape, dtype, name=name, tag=tag or name, align_bytes=64)
+
+        offsets = sb.tile([P, I // 16], U16, name="offsets")
+        nc.sync.dma_start(offsets[:], offs)
+
+        def load_scales(name, scales, clearer, queue):
+            pool_scales = sbuf(name, [P, T], U8)
+            clearer.memset(pool_scales[:].bitcast(I32), 0)
+            for quad in range(4):
+                queue.dma_start(
+                    pool_scales[32 * quad : 32 * quad + 4, :].bitcast(I32),
+                    scales[0, 4 * quad : 4 * quad + 4, :].bitcast(I32),
+                )
+            return pool_scales
+
+        def load_words(name, words):
+            pool_words = sbuf(name, [P, T], U16)
+            nc.sync.dma_start(pool_words[:].bitcast(I32), words[0].bitcast(I32))
+            return pool_words
+
+        def load_rows(name, rows, tag=None):
+            raw = sbuf(name, [P, PACK, Q], F32, tag)
+            nc.sync.dma_start(raw[:], rows.rearrange("(p t) q -> p t q", t=PACK))
+            return raw
+
+        ident = sbuf("ident", [P, P], F32)
+        make_identity(nc, ident[:])
+        ident_bf = sbuf("ident_bf", [P, P], BF16)
+        make_identity(nc, ident_bf[:])
+
+        keys_pool_words = load_words("keys_pool_words", keys_words)
+        query_raw = load_rows("query_raw", query)
+        vals_pool_words = load_words("vals_pool_words", vals_words)
+        keys_pool_scales = load_scales("keys_pool_scales", keys_scales, nc.vector, nc.scalar)
+        vals_pool_scales = load_scales("vals_pool_scales", vals_scales, nc.gpsimd, nc.gpsimd)
+
+        def slot_vector_rows(vec):
+            return vec.rearrange("(b r j) o -> r b (j o)", r=PACK, j=8)
+
+        def four_rows(tile, first):
+            return tile[first : first + PACK, :].rearrange("r (b j) -> r b j", j=8)
+
+        slot_rows = sbuf("slot_rows", [P, P], F32)
+        us_rows = sbuf("us_rows", [P, P], F32)
+        fs_rows = sbuf("fs_rows", [P, P], F32)
+        nc.vector.memset(slot_rows[:], 0.0)
+        nc.gpsimd.dma_start(four_rows(slot_rows, 0), slot_vector_rows(reserve))
+        nc.gpsimd.dma_start(four_rows(us_rows, 32), slot_vector_rows(us))
+        nc.gpsimd.dma_start(four_rows(fs_rows, 32), slot_vector_rows(fs))
+        nc.gpsimd.tensor_tensor(slot_rows[32:36, :], us_rows[32:36, :], fs_rows[32:36, :], ALU.mult)
+
+        def gather_scales(name, pool_scales):
+            listed = sbuf(name + "_listed", [P, I], U8)
+            nc.vector.tensor_copy(listed[:], pool_scales[:].indirect(offsets[:]))
+            dealt = sbuf(name + "_dealt", [P, I], U8)
+            nc.vector.tensor_copy(
+                dealt[:].bitcast(I32).rearrange("p (r b w) -> p r b w", r=PACK, w=2),
+                listed[:].bitcast(I32).rearrange("p (b r w) -> p r b w", r=PACK, w=2),
+            )
+            return dealt
+
+        def gather_words(name, pool_words, tag=None):
+            listed = sbuf(name + "_listed", [P, I], U16, tag)
+            nc.vector.tensor_copy(listed[:], pool_words[:].indirect(offsets[:]))
+            dealt = sbuf(name + "_dealt", [P, 2 * I], U8)
+            nc.vector.tensor_copy(
+                dealt[:].bitcast(U16).rearrange("p (r b j) -> p r b j", r=PACK, j=8),
+                listed[:].rearrange("p (b r j) -> p r b j", r=PACK, j=8),
+            )
+            return dealt
+
+        def quantise_rows(name, raw):
+            grouped = sbuf(name + "_grouped", [P, Q * PACK], BF16)
+            nc.scalar.activation(
+                grouped[:].rearrange("p (c i t) -> p c t i", i=4, t=PACK),
+                raw[:].rearrange("p t (c i) -> p c t i", i=4),
+                ACT.Copy,
+            )
+            codes = sbuf(name + "_codes", [P, Q], U32)
+            scales = sbuf(name + "_scales", [P, Q], U8)
+            nc.vector.quantize_mx(out=codes[:].bitcast(FP8X4), scales=scales[:], in_=grouped[:])
+            return codes, scales
+
+        def slot_products(tag, words, word_scales, codes, scales):
+            banks = []
+            for h in range(2):
+                bank = ps.tile([P, PACK, HALF], F32, name="%s%d" % (tag, h), tag="%s%d" % (tag, h))
+                cols = slice(h * HALF, (h + 1) * HALF)
+                for r in range(PACK):
+                    nc.tensor.matmul_mx(
+                        out=bank[:, r, :],
+                        lhsT=words[:, 2 * P * r : 2 * P * (r + 1)].bitcast(FP4X4),
+                        lhsT_scale=word_scales[:, P * r : P * (r + 1)],
+                        rhs=codes[:, cols].bitcast(FP8X4),
+                        rhs_scale=scales[:, cols],
+                        start=True,
+                        stop=True,
+                    )
+                banks.append(bank)
+            return banks
+
+        def by_member(bank):
+            return bank[:].rearrange("p r (g j) -> p j g r", j=TEAM)
+
+        def half_of(tile, h):
+            return tile[:].rearrange("p j (g r) -> p j g r", r=PACK)[:, :, h * GH : (h + 1) * GH, :]
+
+        keys_s = gather_scales("keys_s", keys_pool_scales)
+        gout_raw = load_rows("gout_raw", gout, "keys_s_listed")
+        keys_w = gather_words("keys_w", keys_pool_words, "keys_pool_scales")
+        query_codes, query_scales = quantise_rows("query", query_raw)
+        vals_s = gather_scales("vals_s", vals_pool_scales)
+        vals_w = gather_words("vals_w", vals_pool_words)
+
+        keyrow_planes = keyrows.rearrange("(p t) c -> t p c", t=PACK)
+        planes = []
+        for t, tag in enumerate(("keys_pool_words", "query_raw", "vals_pool_scales", "vals_pool_words")):
+            plane = sbuf("plane%d" % t, [P, T], F32, tag)
+            nc.sync.dma_start(plane[:], keyrow_planes[t])
+            planes.append(plane)
+        gout_codes, gout_scales = quantise_rows("gout", gout_raw)
+        res_sb = load_rows("res_sb", res, "keys_s_listed")
+
+        a_banks = slot_products("a", keys_w, keys_s, query_codes, query_scales)
+
+        sums = ps.tile([P, 3, P], F32, name="sums")
+        nc.tensor.transpose(sums[:, 2, :], slot_rows[:], ident[:])
+        slot_wide = sbuf("slot_wide", [P, 2, G, PACK], F32)
+        nc.scalar.copy(
+            slot_wide[:],
+            sums[:, 2, 0:64].rearrange("p (v x) -> p v x", v=2)[:, :, 0:PACK].unsqueeze(2).to_broadcast([P, 2, G, PACK]),
+        )
+
+        p = sbuf("p", [P, TEAM, P], F32)
+        for h in range(2):
+            nc.scalar.activation(half_of(p, h), by_member(a_banks[h]), ACT.Exp)
+
+        c_banks = slot_products("c", vals_w, vals_s, gout_codes, gout_scales)
+
+        nc.tensor.matmul(
+            sums[:, 0, :], lhsT=slot_wide[:, 0, :, :].rearrange("p g r -> p (g r)"), rhs=ident[:],
+            is_transpose=True, start=True, stop=False,
+        )
+        for j in range(TEAM):
+            nc.tensor.matmul(
+                sums[:, 0, :], lhsT=p[:, j, :], rhs=ident[:], is_transpose=True, start=False, stop=(j == TEAM - 1)
+            )
+        inv_t = sbuf("inv_t", [P, P], F32)
+        nc.vector.reciprocal(inv_t[:], sums[:, 0, :])
+        nc.tensor.transpose(sums[:, 1, :], inv_t[:], ident[:])
+
+        dbr = sbuf("dbr", [P, TEAM, P], F32)
+        for h in range(2):
+            nc.vector.tensor_tensor(half_of(dbr, h), by_member(c_banks[h]), half_of(p, h), ALU.mult)
+        dsums = ps.tile([P, 2, P], F32, name="dsums")
+        for j in range(TEAM):
+            nc.tensor.matmul(
+                dsums[:, 0, :], lhsT=dbr[:, j, :], rhs=ident[:], is_transpose=True,
+                start=(j == 0), stop=(j == TEAM - 1),
+            )
+        gain = sbuf("gain", [P, G, PACK], F32)
+        nc.vector.tensor_tensor(
+            gain[:],
+            sums[:, 1, :].rearrange("p (g r) -> p g r", r=PACK),
+            slot_wide[:, 1, :, :],
+            ALU.mult,
+        )
+        mean_t = sbuf("mean_t", [P, P], F32)
+        nc.vector.tensor_tensor(mean_t[:], dsums[:, 0, :], inv_t[:], ALU.mult)
+        nc.tensor.transpose(dsums[:, 1, :], mean_t[:], ident[:])
+        mean = sbuf("mean", [P, G, PACK], F32)
+        nc.scalar.copy(mean[:].rearrange("p g r -> p (g r)"), dsums[:, 1, :])
+
+        W = GH * PACK
+        shares = []
+        for h in range(2):
+            share = sbuf("share%d" % h, [P, TEAM, W], F32)
+            nc.gpsimd.tensor_tensor(
+                share[:],
+                p[:, :, h * W : (h + 1) * W],
+                gain[:].rearrange("p g r -> p (g r)")[:, h * W : (h + 1) * W].unsqueeze(1).to_broadcast([P, TEAM, W]),
+                ALU.mult,
+            )
+            shares.append(share)
+
+        kt_codes = sbuf("kt_codes", [P, D], U32)
+        kt_scales = sbuf("kt_scales", [P, D], U8)
+
+        def key_plane(t):
+            listed = sbuf("kr_listed%d" % t, [P, I], BF16)
+            dealt_view = listed[:].rearrange("p (r b j) -> p b r j", r=PACK, j=8)
+            if t == SCALAR_PLANE:
+                rounded = sbuf("kr_rounded%d" % t, [P, T], BF16)
+                nc.scalar.activation(rounded[:], planes[t][:], ACT.Copy)
+                nc.scalar.activation(dealt_view, rounded[:].indirect(offsets[:]), ACT.Copy)
+            else:
+                nc.vector.tensor_copy(dealt_view, planes[t][:].indirect(offsets[:]))
+            turned = ps.tile([P, PACK, P], BF16, name="turned%d" % (t % 2), tag="turned%d" % (t % 2))
+            for r in range(PACK):
+                nc.tensor.transpose(turned[:, r, :], listed[:, P * r : P * (r + 1)], ident_bf[:])
+            grouped = sbuf("kt_grouped%d" % t, [P, P * PACK], BF16)
+            nc.scalar.copy(grouped[:].rearrange("p (m r) -> p m r", r=PACK), turned[:].rearrange("p r m -> p m r"))
+            cols = slice(P * t, P * (t + 1))
+            nc.vector.quantize_mx(out=kt_codes[:, cols].bitcast(FP8X4), scales=kt_scales[:, cols], in_=grouped[:])
+
+        for t in range(PACK):
+            key_plane(t)
+
+        centred = []
+        for h in range(2):
+            x = sbuf("centred%d" % h, [P, GH, TEAM, PACK], F32)
+            nc.vector.tensor_tensor(
+                x[:],
+                c_banks[h][:].rearrange("p r (g j) -> p g j r", j=TEAM),
+                mean[:, h * GH : (h + 1) * GH, :].unsqueeze(2).to_broadcast([P, GH, TEAM, PACK]),
+                ALU.subtract,
+            )
+            centred.append(x)
+        gs_grouped = []
+        for h in range(2):
+            gs = sbuf("gs%d" % h, [P, HALF * PACK], BF16)
+            nc.vector.tensor_tensor(
+                gs[:].rearrange("p (g j r) -> p g j r", j=TEAM, r=PACK),
+                centred[h][:],
+                shares[h][:].rearrange("p j (g r) -> p g j r", r=PACK),
+                ALU.mult,
+            )
+            gs_grouped.append(gs)
+        gq_banks = []
+        for h in range(2):
+            gs_codes = sbuf("gs_codes%d" % h, [P, HALF], U32)
+            gs_scales = sbuf("gs_scales%d" % h, [P, HALF], U8)
+            nc.vector.quantize_mx(out=gs_codes[:].bitcast(FP8X4), scales=gs_scales[:], in_=gs_grouped[h][:])
+            bank = ps.tile([P, PACK, HALF], F32, name="gq%d" % h, tag="a%d" % h)
+            for t in range(PACK):
+                cols = slice(P * t, P * (t + 1))
+                nc.tensor.matmul_mx(
+                    out=bank[:, t, :],
+                    lhsT=kt_codes[:, cols].bitcast(FP8X4),
+                    lhsT_scale=kt_scales[:, cols],
+                    rhs=gs_codes[:].bitcast(FP8X4),
+                    rhs_scale=gs_scales[:],
+                    start=True,
+                    stop=True,
+                )
+            gq_banks.append(bank)
+
+        y_rows = out_0.rearrange("(p t) q -> p t q", t=PACK)
+        y_codes = sbuf("y_codes", [P, Q], U32)
+        y_scales = sbuf("y_scales", [P, Q], U8)
+        y_halves = []
+        for h in range(2):
+            cols = slice(h * HALF, (h + 1) * HALF)
+            y = sbuf("y%d" % h, [P, PACK, HALF], F32)
+            nc.vector.tensor_tensor(y[:], gq_banks[h][:], res_sb[:, :, cols], ALU.add)
+            nc.sync.dma_start(y_rows[:, :, cols], y[:])
+            y_halves.append(y)
+        y_grouped = []
+        for h in range(2):
+            grouped = sbuf("y_grouped%d" % h, [P, HALF * PACK], BF16)
+            dst = grouped[:].rearrange("p (c i t) -> p c t i", i=4, t=PACK)
+            src = y_halves[h][:].rearrange("p t (c i) -> p c t i", i=4)
+            if h == 0:
+                nc.scalar.copy(dst, src)
+            else:
+                nc.vector.tensor_copy(dst, src)
+            y_grouped.append(grouped)
+        for h in range(2):
+            cols = slice(h * HALF, (h + 1) * HALF)
+            nc.vector.quantize_mx(out=y_codes[:, cols].bitcast(FP8X4), scales=y_scales[:, cols], in_=y_grouped[h][:])
+        nc.sync.dma_start(out_1[0].rearrange("p c r -> p (c r)").bitcast(I32), y_codes[:].bitcast(I32))
+        for quad in range(4):
+            queue = nc.scalar if quad % 2 == 0 else nc.sync
+            queue.dma_start(
+                out_2[0, 4 * quad : 4 * quad + 4, :].bitcast(I32),
+                y_scales[32 * quad : 32 * quad + 4, :].bitcast(I32),
+            )

@@ -40,11 +40,12 @@ def tile_attend_bteamshares_q_pl_kernel(
         offsets = sb.tile([P, I // 16], U16, name="offsets")
         nc.sync.dma_start(offsets[:], offs)
 
-        def load_scales(name, scales, clearer, queue):
+        def load_scales(name, scales):
             pool_scales = sbuf(name, [P, T], U8)
-            clearer.memset(pool_scales[:].bitcast(I32), 0)
+            nc.vector.memset(pool_scales[:, : T // 2].bitcast(I32), 0)
+            nc.gpsimd.memset(pool_scales[:, T // 2 :].bitcast(I32), 0)
             for quad in range(4):
-                queue.dma_start(
+                nc.sync.dma_start(
                     pool_scales[32 * quad : 32 * quad + 4, :].bitcast(I32),
                     scales[0, 4 * quad : 4 * quad + 4, :].bitcast(I32),
                 )
@@ -60,61 +61,75 @@ def tile_attend_bteamshares_q_pl_kernel(
             nc.sync.dma_start(raw[:], rows.rearrange("(p t) q -> p t q", t=PACK))
             return raw
 
-        ident = sbuf("ident", [P, P], F32)
-        make_identity(nc, ident[:])
-        ident_bf = sbuf("ident_bf", [P, P], BF16)
-        make_identity(nc, ident_bf[:])
-
-        keys_pool_words = load_words("keys_pool_words", keys_words)
-        query_raw = load_rows("query_raw", query)
-        vals_pool_words = load_words("vals_pool_words", vals_words)
-        keys_pool_scales = load_scales("keys_pool_scales", keys_scales, nc.vector, nc.scalar)
-        vals_pool_scales = load_scales("vals_pool_scales", vals_scales, nc.gpsimd, nc.gpsimd)
-
         def slot_vector_rows(vec):
             return vec.rearrange("(b r j) o -> r b (j o)", r=PACK, j=8)
 
         def four_rows(tile, first):
             return tile[first : first + PACK, :].rearrange("r (b j) -> r b j", j=8)
 
+        keyrow_planes = keyrows.rearrange("(p t) c -> t p c", t=PACK)
+
+        def load_plane(t):
+            plane = sbuf("plane%d" % t, [P, T], F32)
+            nc.sync.dma_start(plane[:], keyrow_planes[t])
+            return plane
+
+        keys_pool_words = load_words("keys_pool_words", keys_words)
+        query_raw = load_rows("query_raw", query)
+        keys_pool_scales = load_scales("keys_pool_scales", keys_scales)
+        vals_pool_words = load_words("vals_pool_words", vals_words)
+        gout_raw = load_rows("gout_raw", gout)
+        vals_pool_scales = load_scales("vals_pool_scales", vals_scales)
         slot_rows = sbuf("slot_rows", [P, P], F32)
         us_rows = sbuf("us_rows", [P, P], F32)
         fs_rows = sbuf("fs_rows", [P, P], F32)
-        nc.vector.memset(slot_rows[:], 0.0)
-        nc.gpsimd.dma_start(four_rows(slot_rows, 0), slot_vector_rows(reserve))
-        nc.gpsimd.dma_start(four_rows(us_rows, 32), slot_vector_rows(us))
-        nc.gpsimd.dma_start(four_rows(fs_rows, 32), slot_vector_rows(fs))
-        nc.gpsimd.tensor_tensor(slot_rows[32:36, :], us_rows[32:36, :], fs_rows[32:36, :], ALU.mult)
+        nc.gpsimd.memset(slot_rows[:], 0.0)
+        nc.sync.dma_start(four_rows(slot_rows, 0), slot_vector_rows(reserve))
+        planes = [load_plane(0)]
+        nc.sync.dma_start(four_rows(us_rows, 32), slot_vector_rows(us))
+        nc.sync.dma_start(four_rows(fs_rows, 32), slot_vector_rows(fs))
+        for t in range(1, PACK):
+            planes.append(load_plane(t))
+        res_sb = load_rows("res_sb", res)
 
-        def gather_scales(name, pool_scales):
-            listed = sbuf(name + "_listed", [P, I], U8)
-            nc.vector.tensor_copy(listed[:], pool_scales[:].indirect(offsets[:]))
-            dealt = sbuf(name + "_dealt", [P, I], U8)
+        ident = sbuf("ident", [P, P], F32)
+        make_identity(nc, ident[:])
+        ident_bf = sbuf("ident_bf", [P, P], BF16)
+        nc.scalar.activation(ident_bf[:], ident[:], ACT.Copy)
+
+        def gather(name, pool_tile, dtype):
+            listed = sbuf(name + "_listed", [P, I], dtype)
+            nc.vector.tensor_copy(listed[:], pool_tile[:].indirect(offsets[:]))
+            return listed
+
+        def deal_scales(name, listed, tag):
+            dealt = sbuf(name + "_dealt", [P, I], U8, tag)
             nc.vector.tensor_copy(
                 dealt[:].bitcast(I32).rearrange("p (r b w) -> p r b w", r=PACK, w=2),
                 listed[:].bitcast(I32).rearrange("p (b r w) -> p r b w", r=PACK, w=2),
             )
             return dealt
 
-        def gather_words(name, pool_words, tag=None):
-            listed = sbuf(name + "_listed", [P, I], U16, tag)
-            nc.vector.tensor_copy(listed[:], pool_words[:].indirect(offsets[:]))
-            dealt = sbuf(name + "_dealt", [P, 2 * I], U8)
+        def deal_words(name, listed, tag):
+            dealt = sbuf(name + "_dealt", [P, 2 * I], U8, tag)
             nc.vector.tensor_copy(
                 dealt[:].bitcast(U16).rearrange("p (r b j) -> p r b j", r=PACK, j=8),
                 listed[:].rearrange("p (b r j) -> p r b j", r=PACK, j=8),
             )
             return dealt
 
-        def quantise_rows(name, raw):
+        def group_rows(name, raw):
             grouped = sbuf(name + "_grouped", [P, Q * PACK], BF16)
             nc.scalar.activation(
                 grouped[:].rearrange("p (c i t) -> p c t i", i=4, t=PACK),
                 raw[:].rearrange("p t (c i) -> p c t i", i=4),
                 ACT.Copy,
             )
-            codes = sbuf(name + "_codes", [P, Q], U32)
-            scales = sbuf(name + "_scales", [P, Q], U8)
+            return grouped
+
+        def quantise(name, grouped, width):
+            codes = sbuf(name + "_codes", [P, width], U32)
+            scales = sbuf(name + "_scales", [P, width], U8)
             nc.vector.quantize_mx(out=codes[:].bitcast(FP8X4), scales=scales[:], in_=grouped[:])
             return codes, scales
 
@@ -142,54 +157,54 @@ def tile_attend_bteamshares_q_pl_kernel(
         def half_of(tile, h):
             return tile[:].rearrange("p j (g r) -> p j g r", r=PACK)[:, :, h * GH : (h + 1) * GH, :]
 
-        keys_s = gather_scales("keys_s", keys_pool_scales)
-        gout_raw = load_rows("gout_raw", gout, "keys_s_listed")
-        keys_w = gather_words("keys_w", keys_pool_words, "keys_pool_scales")
-        query_codes, query_scales = quantise_rows("query", query_raw)
-        vals_s = gather_scales("vals_s", vals_pool_scales)
-        vals_w = gather_words("vals_w", vals_pool_words)
-
-        keyrow_planes = keyrows.rearrange("(p t) c -> t p c", t=PACK)
-        planes = []
-        for t, tag in enumerate(("keys_pool_words", "query_raw", "vals_pool_scales", "vals_pool_words")):
-            plane = sbuf("plane%d" % t, [P, T], F32, tag)
-            nc.sync.dma_start(plane[:], keyrow_planes[t])
-            planes.append(plane)
-        gout_codes, gout_scales = quantise_rows("gout", gout_raw)
-        res_sb = load_rows("res_sb", res, "keys_s_listed")
+        keys_w_listed = gather("keys_w", keys_pool_words, U16)
+        keys_s_listed = gather("keys_s", keys_pool_scales, U8)
+        vals_w_listed = gather("vals_w", vals_pool_words, U16)
+        query_grouped = group_rows("query", query_raw)
+        keys_w = deal_words("keys_w", keys_w_listed, "query_raw")
+        query_codes, query_scales = quantise("query", query_grouped, Q)
+        keys_s = deal_scales("keys_s", keys_s_listed, "keys_w_listed")
+        vals_s_listed = gather("vals_s", vals_pool_scales, U8)
+        gout_grouped = group_rows("gout", gout_raw)
+        vals_w = deal_words("vals_w", vals_w_listed, "gout_raw")
+        gout_codes, gout_scales = quantise("gout", gout_grouped, Q)
+        vals_s = deal_scales("vals_s", vals_s_listed, "vals_w_listed")
 
         a_banks = slot_products("a", keys_w, keys_s, query_codes, query_scales)
-
-        sums = ps.tile([P, 3, P], F32, name="sums")
-        nc.tensor.transpose(sums[:, 2, :], slot_rows[:], ident[:])
-        slot_wide = sbuf("slot_wide", [P, 2, G, PACK], F32)
-        nc.scalar.copy(
-            slot_wide[:],
-            sums[:, 2, 0:64].rearrange("p (v x) -> p v x", v=2)[:, :, 0:PACK].unsqueeze(2).to_broadcast([P, 2, G, PACK]),
-        )
 
         p = sbuf("p", [P, TEAM, P], F32)
         for h in range(2):
             nc.scalar.activation(half_of(p, h), by_member(a_banks[h]), ACT.Exp)
 
-        c_banks = slot_products("c", vals_w, vals_s, gout_codes, gout_scales)
+        def spread_over_teams(name, turned_rows):
+            wide = sbuf(name, [P, G, PACK], F32)
+            nc.scalar.copy(wide[:], turned_rows.unsqueeze(1).to_broadcast([P, G, PACK]))
+            return wide
 
+        sums = ps.tile([P, 3, P], F32, name="sums")
+        nc.tensor.transpose(sums[:, 2, :], slot_rows[:], ident[:])
+        reserve_wide = spread_over_teams("reserve_wide", sums[:, 2, 0:PACK])
         nc.tensor.matmul(
-            sums[:, 0, :], lhsT=slot_wide[:, 0, :, :].rearrange("p g r -> p (g r)"), rhs=ident[:],
+            sums[:, 0, :], lhsT=reserve_wide[:].rearrange("p g r -> p (g r)"), rhs=ident[:],
             is_transpose=True, start=True, stop=False,
         )
         for j in range(TEAM):
             nc.tensor.matmul(
                 sums[:, 0, :], lhsT=p[:, j, :], rhs=ident[:], is_transpose=True, start=False, stop=(j == TEAM - 1)
             )
+        c_banks = slot_products("c", vals_w, vals_s, gout_codes, gout_scales)
         inv_t = sbuf("inv_t", [P, P], F32)
         nc.vector.reciprocal(inv_t[:], sums[:, 0, :])
         nc.tensor.transpose(sums[:, 1, :], inv_t[:], ident[:])
 
+        dsums = ps.tile([P, 3, P], F32, name="dsums")
+        nc.vector.tensor_tensor(slot_rows[32:36, :], us_rows[32:36, :], fs_rows[32:36, :], ALU.mult)
+        nc.tensor.transpose(dsums[:, 2, :], slot_rows[:], ident[:])
+        usfs_wide = spread_over_teams("usfs_wide", dsums[:, 2, 32 : 32 + PACK])
+
         dbr = sbuf("dbr", [P, TEAM, P], F32)
         for h in range(2):
             nc.vector.tensor_tensor(half_of(dbr, h), by_member(c_banks[h]), half_of(p, h), ALU.mult)
-        dsums = ps.tile([P, 2, P], F32, name="dsums")
         for j in range(TEAM):
             nc.tensor.matmul(
                 dsums[:, 0, :], lhsT=dbr[:, j, :], rhs=ident[:], is_transpose=True,
@@ -199,7 +214,7 @@ def tile_attend_bteamshares_q_pl_kernel(
         nc.vector.tensor_tensor(
             gain[:],
             sums[:, 1, :].rearrange("p (g r) -> p g r", r=PACK),
-            slot_wide[:, 1, :, :],
+            usfs_wide[:],
             ALU.mult,
         )
         mean_t = sbuf("mean_t", [P, P], F32)
@@ -212,7 +227,7 @@ def tile_attend_bteamshares_q_pl_kernel(
         shares = []
         for h in range(2):
             share = sbuf("share%d" % h, [P, TEAM, W], F32)
-            nc.gpsimd.tensor_tensor(
+            nc.vector.tensor_tensor(
                 share[:],
                 p[:, :, h * W : (h + 1) * W],
                 gain[:].rearrange("p g r -> p (g r)")[:, h * W : (h + 1) * W].unsqueeze(1).to_broadcast([P, TEAM, W]),
@@ -220,8 +235,7 @@ def tile_attend_bteamshares_q_pl_kernel(
             )
             shares.append(share)
 
-        kt_codes = sbuf("kt_codes", [P, D], U32)
-        kt_scales = sbuf("kt_scales", [P, D], U8)
+        kt_grouped = sbuf("kt_grouped", [P, D * PACK], BF16)
 
         def key_plane(t):
             listed = sbuf("kr_listed%d" % t, [P, I], BF16)
@@ -235,39 +249,36 @@ def tile_attend_bteamshares_q_pl_kernel(
             turned = ps.tile([P, PACK, P], BF16, name="turned%d" % (t % 2), tag="turned%d" % (t % 2))
             for r in range(PACK):
                 nc.tensor.transpose(turned[:, r, :], listed[:, P * r : P * (r + 1)], ident_bf[:])
-            grouped = sbuf("kt_grouped%d" % t, [P, P * PACK], BF16)
-            nc.scalar.copy(grouped[:].rearrange("p (m r) -> p m r", r=PACK), turned[:].rearrange("p r m -> p m r"))
-            cols = slice(P * t, P * (t + 1))
-            nc.vector.quantize_mx(out=kt_codes[:, cols].bitcast(FP8X4), scales=kt_scales[:, cols], in_=grouped[:])
+            nc.scalar.copy(
+                kt_grouped[:, P * PACK * t : P * PACK * (t + 1)].rearrange("p (m r) -> p m r", r=PACK),
+                turned[:].rearrange("p r m -> p m r"),
+            )
 
         for t in range(PACK):
             key_plane(t)
+        kt_codes, kt_scales = quantise("kt", kt_grouped, D)
 
-        centred = []
+        centred = sbuf("centred", [P, 2, GH, TEAM, PACK], F32, "plane%d" % (PACK - 1))
         for h in range(2):
-            x = sbuf("centred%d" % h, [P, GH, TEAM, PACK], F32)
             nc.vector.tensor_tensor(
-                x[:],
+                centred[:, h],
                 c_banks[h][:].rearrange("p r (g j) -> p g j r", j=TEAM),
                 mean[:, h * GH : (h + 1) * GH, :].unsqueeze(2).to_broadcast([P, GH, TEAM, PACK]),
                 ALU.subtract,
             )
-            centred.append(x)
         gs_grouped = []
         for h in range(2):
             gs = sbuf("gs%d" % h, [P, HALF * PACK], BF16)
             nc.vector.tensor_tensor(
                 gs[:].rearrange("p (g j r) -> p g j r", j=TEAM, r=PACK),
-                centred[h][:],
+                centred[:, h],
                 shares[h][:].rearrange("p j (g r) -> p g j r", r=PACK),
                 ALU.mult,
             )
             gs_grouped.append(gs)
         gq_banks = []
         for h in range(2):
-            gs_codes = sbuf("gs_codes%d" % h, [P, HALF], U32)
-            gs_scales = sbuf("gs_scales%d" % h, [P, HALF], U8)
-            nc.vector.quantize_mx(out=gs_codes[:].bitcast(FP8X4), scales=gs_scales[:], in_=gs_grouped[h][:])
+            gs_codes, gs_scales = quantise("gs%d" % h, gs_grouped[h], HALF)
             bank = ps.tile([P, PACK, HALF], F32, name="gq%d" % h, tag="a%d" % h)
             for t in range(PACK):
                 cols = slice(P * t, P * (t + 1))

@@ -22,7 +22,7 @@ PACK = 4
 TEAM = Q // G
 HALF = Q // 2
 GH = G // 2
-SCALAR_PLANE = 1
+SCALAR_PLANES = (1, 2)
 
 
 def tile_attend_bteamshares_q_pl_kernel(
@@ -46,8 +46,8 @@ def tile_attend_bteamshares_q_pl_kernel(
             nc.gpsimd.memset(pool_scales[:, T // 2 :].bitcast(I32), 0)
             for quad in range(4):
                 nc.sync.dma_start(
-                    pool_scales[32 * quad : 32 * quad + 4, :].bitcast(I32),
-                    scales[0, 4 * quad : 4 * quad + 4, :].bitcast(I32),
+                    pool_scales[quad:P:32, :].bitcast(I32),
+                    scales[0].rearrange("(b r) c -> r b c", r=4)[quad].bitcast(I32),
                 )
             return pool_scales
 
@@ -61,11 +61,10 @@ def tile_attend_bteamshares_q_pl_kernel(
             nc.sync.dma_start(raw[:], rows.rearrange("(p t) q -> p t q", t=PACK))
             return raw
 
-        def slot_vector_rows(vec):
-            return vec.rearrange("(b r j) o -> r b (j o)", r=PACK, j=8)
-
-        def four_rows(tile, first):
-            return tile[first : first + PACK, :].rearrange("r (b j) -> r b j", j=8)
+        def load_slot_vector(name, vec):
+            cols = sbuf(name, [P, PACK], F32)
+            nc.sync.dma_start(cols[:], vec.rearrange("(p r) o -> p (r o)", r=PACK))
+            return cols
 
         keyrow_planes = keyrows.rearrange("(p t) c -> t p c", t=PACK)
 
@@ -80,22 +79,16 @@ def tile_attend_bteamshares_q_pl_kernel(
         vals_pool_words = load_words("vals_pool_words", vals_words)
         gout_raw = load_rows("gout_raw", gout)
         vals_pool_scales = load_scales("vals_pool_scales", vals_scales)
-        slot_rows = sbuf("slot_rows", [P, P], F32)
-        us_rows = sbuf("us_rows", [P, P], F32)
-        fs_rows = sbuf("fs_rows", [P, P], F32)
-        nc.gpsimd.memset(slot_rows[:], 0.0)
-        nc.sync.dma_start(four_rows(slot_rows, 0), slot_vector_rows(reserve))
+        reserve_cols = load_slot_vector("reserve_cols", reserve)
         planes = [load_plane(0)]
-        nc.sync.dma_start(four_rows(us_rows, 32), slot_vector_rows(us))
-        nc.sync.dma_start(four_rows(fs_rows, 32), slot_vector_rows(fs))
+        us_cols = load_slot_vector("us_cols", us)
+        fs_cols = load_slot_vector("fs_cols", fs)
         for t in range(1, PACK):
             planes.append(load_plane(t))
         res_sb = load_rows("res_sb", res)
 
         ident = sbuf("ident", [P, P], F32)
         make_identity(nc, ident[:])
-        ident_bf = sbuf("ident_bf", [P, P], BF16)
-        nc.scalar.activation(ident_bf[:], ident[:], ACT.Copy)
 
         def gather(name, pool_tile, dtype):
             listed = sbuf(name + "_listed", [P, I], dtype)
@@ -105,16 +98,16 @@ def tile_attend_bteamshares_q_pl_kernel(
         def deal_scales(name, listed, tag):
             dealt = sbuf(name + "_dealt", [P, I], U8, tag)
             nc.vector.tensor_copy(
-                dealt[:].bitcast(I32).rearrange("p (r b w) -> p r b w", r=PACK, w=2),
-                listed[:].bitcast(I32).rearrange("p (b r w) -> p r b w", r=PACK, w=2),
+                dealt[:].rearrange("p (r s) -> p r s", r=PACK),
+                listed[:].rearrange("p (s r) -> p r s", r=PACK),
             )
             return dealt
 
         def deal_words(name, listed, tag):
             dealt = sbuf(name + "_dealt", [P, 2 * I], U8, tag)
             nc.vector.tensor_copy(
-                dealt[:].bitcast(U16).rearrange("p (r b j) -> p r b j", r=PACK, j=8),
-                listed[:].rearrange("p (b r j) -> p r b j", r=PACK, j=8),
+                dealt[:].bitcast(U16).rearrange("p (r s) -> p r s", r=PACK),
+                listed[:].rearrange("p (s r) -> p r s", r=PACK),
             )
             return dealt
 
@@ -152,18 +145,18 @@ def tile_attend_bteamshares_q_pl_kernel(
             return banks
 
         def by_member(bank):
-            return bank[:].rearrange("p r (g j) -> p j g r", j=TEAM)
+            return bank[:].rearrange("p r (g j) -> p g j r", j=TEAM)
 
         def half_of(tile, h):
-            return tile[:].rearrange("p j (g r) -> p j g r", r=PACK)[:, :, h * GH : (h + 1) * GH, :]
+            return tile[:].rearrange("p j (g r) -> p g j r", r=PACK)[:, h * GH : (h + 1) * GH, :, :]
 
         keys_w_listed = gather("keys_w", keys_pool_words, U16)
         keys_s_listed = gather("keys_s", keys_pool_scales, U8)
-        vals_w_listed = gather("vals_w", vals_pool_words, U16)
         query_grouped = group_rows("query", query_raw)
         keys_w = deal_words("keys_w", keys_w_listed, "query_raw")
         query_codes, query_scales = quantise("query", query_grouped, Q)
         keys_s = deal_scales("keys_s", keys_s_listed, "keys_w_listed")
+        vals_w_listed = gather("vals_w", vals_pool_words, U16)
         vals_s_listed = gather("vals_s", vals_pool_scales, U8)
         gout_grouped = group_rows("gout", gout_raw)
         vals_w = deal_words("vals_w", vals_w_listed, "gout_raw")
@@ -176,14 +169,9 @@ def tile_attend_bteamshares_q_pl_kernel(
         for h in range(2):
             nc.scalar.activation(half_of(p, h), by_member(a_banks[h]), ACT.Exp)
 
-        def spread_over_teams(name, turned_rows):
-            wide = sbuf(name, [P, G, PACK], F32)
-            nc.scalar.copy(wide[:], turned_rows.unsqueeze(1).to_broadcast([P, G, PACK]))
-            return wide
-
-        sums = ps.tile([P, 3, P], F32, name="sums")
-        nc.tensor.transpose(sums[:, 2, :], slot_rows[:], ident[:])
-        reserve_wide = spread_over_teams("reserve_wide", sums[:, 2, 0:PACK])
+        reserve_wide = sbuf("reserve_wide", [P, G, PACK], F32)
+        nc.scalar.copy(reserve_wide[:], reserve_cols[:].unsqueeze(1).to_broadcast([P, G, PACK]))
+        sums = ps.tile([P, 2, P], F32, name="sums")
         nc.tensor.matmul(
             sums[:, 0, :], lhsT=reserve_wide[:].rearrange("p g r -> p (g r)"), rhs=ident[:],
             is_transpose=True, start=True, stop=False,
@@ -193,14 +181,25 @@ def tile_attend_bteamshares_q_pl_kernel(
                 sums[:, 0, :], lhsT=p[:, j, :], rhs=ident[:], is_transpose=True, start=False, stop=(j == TEAM - 1)
             )
         c_banks = slot_products("c", vals_w, vals_s, gout_codes, gout_scales)
-        inv_t = sbuf("inv_t", [P, P], F32)
+
+        def gather_plane(t):
+            listed = sbuf("kr_listed%d" % t, [P, I], BF16)
+            if t in SCALAR_PLANES:
+                rounded = sbuf("kr_rounded%d" % t, [P, T], BF16)
+                nc.scalar.activation(rounded[:], planes[t][:], ACT.Copy)
+                nc.scalar.activation(listed[:], rounded[:].indirect(offsets[:]), ACT.Copy)
+            else:
+                nc.vector.tensor_copy(listed[:], planes[t][:].indirect(offsets[:]))
+            return listed
+
+        listed_planes = [gather_plane(0)]
+        inv_t = sbuf("inv_t", [P, P], F32, "plane0")
         nc.vector.reciprocal(inv_t[:], sums[:, 0, :])
         nc.tensor.transpose(sums[:, 1, :], inv_t[:], ident[:])
 
-        dsums = ps.tile([P, 3, P], F32, name="dsums")
-        nc.vector.tensor_tensor(slot_rows[32:36, :], us_rows[32:36, :], fs_rows[32:36, :], ALU.mult)
-        nc.tensor.transpose(dsums[:, 2, :], slot_rows[:], ident[:])
-        usfs_wide = spread_over_teams("usfs_wide", dsums[:, 2, 32 : 32 + PACK])
+        dsums = ps.tile([P, 2, P], F32, name="dsums")
+        usfs = sbuf("usfs", [P, PACK], F32)
+        nc.vector.tensor_tensor(usfs[:], us_cols[:], fs_cols[:], ALU.mult)
 
         dbr = sbuf("dbr", [P, TEAM, P], F32)
         for h in range(2):
@@ -214,71 +213,58 @@ def tile_attend_bteamshares_q_pl_kernel(
         nc.vector.tensor_tensor(
             gain[:],
             sums[:, 1, :].rearrange("p (g r) -> p g r", r=PACK),
-            usfs_wide[:],
+            usfs[:].unsqueeze(1).to_broadcast([P, G, PACK]),
             ALU.mult,
+        )
+        share = sbuf("share", [P, TEAM, P], F32)
+        nc.vector.tensor_tensor(
+            share[:], p[:], gain[:].rearrange("p g r -> p (g r)").unsqueeze(1).to_broadcast([P, TEAM, P]), ALU.mult
         )
         mean_t = sbuf("mean_t", [P, P], F32)
         nc.vector.tensor_tensor(mean_t[:], dsums[:, 0, :], inv_t[:], ALU.mult)
         nc.tensor.transpose(dsums[:, 1, :], mean_t[:], ident[:])
-        mean = sbuf("mean", [P, G, PACK], F32)
-        nc.scalar.copy(mean[:].rearrange("p g r -> p (g r)"), dsums[:, 1, :])
 
-        W = GH * PACK
-        shares = []
-        for h in range(2):
-            share = sbuf("share%d" % h, [P, TEAM, W], F32)
-            nc.vector.tensor_tensor(
-                share[:],
-                p[:, :, h * W : (h + 1) * W],
-                gain[:].rearrange("p g r -> p (g r)")[:, h * W : (h + 1) * W].unsqueeze(1).to_broadcast([P, TEAM, W]),
-                ALU.mult,
-            )
-            shares.append(share)
+        for t in range(1, PACK):
+            listed_planes.append(gather_plane(t))
+        mean = sbuf("mean", [P, G, PACK], F32, "plane%d" % (PACK - 1))
+        nc.vector.tensor_copy(mean[:].rearrange("p g r -> p (g r)"), dsums[:, 1, :])
+        kt_grouped = sbuf("kt_grouped", [P, D * PACK], BF16, "kr_rounded%d" % SCALAR_PLANES[-1])
 
-        kt_grouped = sbuf("kt_grouped", [P, D * PACK], BF16)
-
-        def key_plane(t):
-            listed = sbuf("kr_listed%d" % t, [P, I], BF16)
-            dealt_view = listed[:].rearrange("p (r b j) -> p b r j", r=PACK, j=8)
-            if t == SCALAR_PLANE:
-                rounded = sbuf("kr_rounded%d" % t, [P, T], BF16)
-                nc.scalar.activation(rounded[:], planes[t][:], ACT.Copy)
-                nc.scalar.activation(dealt_view, rounded[:].indirect(offsets[:]), ACT.Copy)
-            else:
-                nc.vector.tensor_copy(dealt_view, planes[t][:].indirect(offsets[:]))
-            turned = ps.tile([P, PACK, P], BF16, name="turned%d" % (t % 2), tag="turned%d" % (t % 2))
-            for r in range(PACK):
-                nc.tensor.transpose(turned[:, r, :], listed[:, P * r : P * (r + 1)], ident_bf[:])
+        def turn_plane(t):
+            pairs = listed_planes[t][:].bitcast(F32)
+            turned = ps.tile([P, 2, P], F32, name="turned%d" % t, tag=("sums", "turned1", "turned2", "dsums")[t])
+            for u in range(2):
+                nc.tensor.transpose(turned[:, u, :], pairs[:, u : I // 2 : 2], ident[:])
             nc.scalar.copy(
-                kt_grouped[:, P * PACK * t : P * PACK * (t + 1)].rearrange("p (m r) -> p m r", r=PACK),
-                turned[:].rearrange("p r m -> p m r"),
+                kt_grouped[:, P * PACK * t : P * PACK * (t + 1)].bitcast(F32).rearrange("p (m u) -> p m u", u=2),
+                turned[:].rearrange("p u m -> p m u"),
             )
 
         for t in range(PACK):
-            key_plane(t)
-        kt_codes, kt_scales = quantise("kt", kt_grouped, D)
+            turn_plane(t)
 
-        centred = sbuf("centred", [P, 2, GH, TEAM, PACK], F32, "plane%d" % (PACK - 1))
+        centred = sbuf("centred", [P, 2, GH, TEAM, PACK], F32)
         for h in range(2):
             nc.vector.tensor_tensor(
                 centred[:, h],
-                c_banks[h][:].rearrange("p r (g j) -> p g j r", j=TEAM),
+                by_member(c_banks[h]),
                 mean[:, h * GH : (h + 1) * GH, :].unsqueeze(2).to_broadcast([P, GH, TEAM, PACK]),
                 ALU.subtract,
             )
-        gs_grouped = []
-        for h in range(2):
+
+        def score_gradient(h):
             gs = sbuf("gs%d" % h, [P, HALF * PACK], BF16)
             nc.vector.tensor_tensor(
-                gs[:].rearrange("p (g j r) -> p g j r", j=TEAM, r=PACK),
-                centred[:, h],
-                shares[h][:].rearrange("p j (g r) -> p g j r", r=PACK),
-                ALU.mult,
+                gs[:].rearrange("p (g j r) -> p g j r", j=TEAM, r=PACK), centred[:, h], half_of(share, h), ALU.mult
             )
-            gs_grouped.append(gs)
+            return quantise("gs%d" % h, gs, HALF)
+
+        gs_halves = [score_gradient(0)]
+        kt_codes, kt_scales = quantise("kt", kt_grouped, D)
+        gs_halves.append(score_gradient(1))
         gq_banks = []
         for h in range(2):
-            gs_codes, gs_scales = quantise("gs%d" % h, gs_grouped[h], HALF)
+            gs_codes, gs_scales = gs_halves[h]
             bank = ps.tile([P, PACK, HALF], F32, name="gq%d" % h, tag="a%d" % h)
             for t in range(PACK):
                 cols = slice(P * t, P * (t + 1))
@@ -294,32 +280,26 @@ def tile_attend_bteamshares_q_pl_kernel(
             gq_banks.append(bank)
 
         y_rows = out_0.rearrange("(p t) q -> p t q", t=PACK)
-        y_codes = sbuf("y_codes", [P, Q], U32)
-        y_scales = sbuf("y_scales", [P, Q], U8)
         y_halves = []
         for h in range(2):
             cols = slice(h * HALF, (h + 1) * HALF)
-            y = sbuf("y%d" % h, [P, PACK, HALF], F32)
+            y = sbuf("y%d" % h, [P, PACK, HALF], F32, "gs%d" % (1 - h))
             nc.vector.tensor_tensor(y[:], gq_banks[h][:], res_sb[:, :, cols], ALU.add)
             nc.sync.dma_start(y_rows[:, :, cols], y[:])
             y_halves.append(y)
-        y_grouped = []
+        y_grouped = sbuf("y_grouped", [P, Q * PACK], BF16)
         for h in range(2):
-            grouped = sbuf("y_grouped%d" % h, [P, HALF * PACK], BF16)
-            dst = grouped[:].rearrange("p (c i t) -> p c t i", i=4, t=PACK)
+            dst = y_grouped[:, h * HALF * PACK : (h + 1) * HALF * PACK].rearrange("p (c i t) -> p c t i", i=4, t=PACK)
             src = y_halves[h][:].rearrange("p t (c i) -> p c t i", i=4)
             if h == 0:
                 nc.scalar.copy(dst, src)
             else:
                 nc.vector.tensor_copy(dst, src)
-            y_grouped.append(grouped)
-        for h in range(2):
-            cols = slice(h * HALF, (h + 1) * HALF)
-            nc.vector.quantize_mx(out=y_codes[:, cols].bitcast(FP8X4), scales=y_scales[:, cols], in_=y_grouped[h][:])
+        y_codes, y_scales = quantise("y", y_grouped, Q)
         nc.sync.dma_start(out_1[0].rearrange("p c r -> p (c r)").bitcast(I32), y_codes[:].bitcast(I32))
         for quad in range(4):
             queue = nc.scalar if quad % 2 == 0 else nc.sync
             queue.dma_start(
-                out_2[0, 4 * quad : 4 * quad + 4, :].bitcast(I32),
-                y_scales[32 * quad : 32 * quad + 4, :].bitcast(I32),
+                out_2[0].rearrange("(b r) c -> r b c", r=4)[quad].bitcast(I32),
+                y_scales[quad:P:32, :].bitcast(I32),
             )

@@ -37,8 +37,6 @@ def tile_attend_bteamshares_q_pl_kernel(
         def sbuf(name, shape, dtype, tag=None):
             return sb.tile(shape, dtype, name=name, tag=tag or name, align_bytes=64)
 
-        offsets = sb.tile([P, I // 16], U16, name="offsets")
-        nc.sync.dma_start(offsets[:], offs)
 
         def load_scales(name, scales):
             pool_scales = sbuf(name, [P, T], U8)
@@ -74,6 +72,8 @@ def tile_attend_bteamshares_q_pl_kernel(
             return plane
 
         keys_pool_words = load_words("keys_pool_words", keys_words)
+        offsets = sb.tile([P, I // 16], U16, name="offsets")
+        nc.sync.dma_start(offsets[:], offs)
         query_raw = load_rows("query_raw", query)
         keys_pool_scales = load_scales("keys_pool_scales", keys_scales)
         vals_pool_words = load_words("vals_pool_words", vals_words)
@@ -120,8 +120,8 @@ def tile_attend_bteamshares_q_pl_kernel(
             )
             return grouped
 
-        def quantise(name, grouped, width):
-            codes = sbuf(name + "_codes", [P, width], U32)
+        def quantise(name, grouped, width, tag=None):
+            codes = sbuf(name + "_codes", [P, width], U32, tag)
             scales = sbuf(name + "_scales", [P, width], U8)
             nc.vector.quantize_mx(out=codes[:].bitcast(FP8X4), scales=scales[:], in_=grouped[:])
             return codes, scales
@@ -159,27 +159,25 @@ def tile_attend_bteamshares_q_pl_kernel(
         vals_w_listed = gather("vals_w", vals_pool_words, U16)
         vals_s_listed = gather("vals_s", vals_pool_scales, U8)
         gout_grouped = group_rows("gout", gout_raw)
-        vals_w = deal_words("vals_w", vals_w_listed, "gout_raw")
-        gout_codes, gout_scales = quantise("gout", gout_grouped, Q)
+        vals_w = deal_words("vals_w", vals_w_listed, "vals_pool_scales")
         vals_s = deal_scales("vals_s", vals_s_listed, "vals_w_listed")
 
         a_banks = slot_products("a", keys_w, keys_s, query_codes, query_scales)
 
-        p = sbuf("p", [P, TEAM, P], F32)
+        p = sbuf("p", [P, TEAM, P], F32, "gout_raw")
         for h in range(2):
             nc.scalar.activation(half_of(p, h), by_member(a_banks[h]), ACT.Exp)
 
         reserve_wide = sbuf("reserve_wide", [P, G, PACK], F32)
         nc.scalar.copy(reserve_wide[:], reserve_cols[:].unsqueeze(1).to_broadcast([P, G, PACK]))
         sums = ps.tile([P, 2, P], F32, name="sums")
-        nc.tensor.matmul(
-            sums[:, 0, :], lhsT=reserve_wide[:].rearrange("p g r -> p (g r)"), rhs=ident[:],
-            is_transpose=True, start=True, stop=False,
-        )
-        for j in range(TEAM):
+        members = [p[:, j, :] for j in range(TEAM)]
+        terms = members[:1] + [reserve_wide[:].rearrange("p g r -> p (g r)")] + members[1:]
+        for n, term in enumerate(terms):
             nc.tensor.matmul(
-                sums[:, 0, :], lhsT=p[:, j, :], rhs=ident[:], is_transpose=True, start=False, stop=(j == TEAM - 1)
+                sums[:, 0, :], lhsT=term, rhs=ident[:], is_transpose=True, start=(n == 0), stop=(n == TEAM)
             )
+        gout_codes, gout_scales = quantise("gout", gout_grouped, Q, "reserve_wide")
         c_banks = slot_products("c", vals_w, vals_s, gout_codes, gout_scales)
 
         def gather_plane(t):
@@ -193,15 +191,15 @@ def tile_attend_bteamshares_q_pl_kernel(
             return listed
 
         listed_planes = [gather_plane(0)]
-        inv_t = sbuf("inv_t", [P, P], F32, "plane0")
+        usfs = sbuf("usfs", [P, PACK], F32)
+        nc.vector.tensor_tensor(usfs[:], us_cols[:], fs_cols[:], ALU.mult)
+        inv_t = sbuf("inv_t", [P, P], F32, "us_cols")
         nc.vector.reciprocal(inv_t[:], sums[:, 0, :])
         nc.tensor.transpose(sums[:, 1, :], inv_t[:], ident[:])
 
         dsums = ps.tile([P, 2, P], F32, name="dsums")
-        usfs = sbuf("usfs", [P, PACK], F32)
-        nc.vector.tensor_tensor(usfs[:], us_cols[:], fs_cols[:], ALU.mult)
 
-        dbr = sbuf("dbr", [P, TEAM, P], F32)
+        dbr = sbuf("dbr", [P, TEAM, P], F32, "fs_cols")
         for h in range(2):
             nc.vector.tensor_tensor(half_of(dbr, h), by_member(c_banks[h]), half_of(p, h), ALU.mult)
         for j in range(TEAM):
@@ -257,17 +255,24 @@ def tile_attend_bteamshares_q_pl_kernel(
             nc.vector.tensor_tensor(
                 gs[:].rearrange("p (g j r) -> p g j r", j=TEAM, r=PACK), centred[:, h], half_of(share, h), ALU.mult
             )
-            return quantise("gs%d" % h, gs, HALF)
+            return gs
 
-        gs_halves = [score_gradient(0)]
-        kt_codes, kt_scales = quantise("kt", kt_grouped, D)
-        gs_halves.append(score_gradient(1))
+        def quantise_key_pair(pair, tag):
+            width = 2 * P
+            return quantise("kt%d" % pair, kt_grouped[:, pair * width * PACK : (pair + 1) * width * PACK], width, tag)
+
+        gs_first = score_gradient(0)
+        kt_pairs = [quantise_key_pair(0, "plane%d" % (PACK - 1))]
+        gs_halves = [quantise("gs0", gs_first, HALF)]
+        kt_pairs.append(quantise_key_pair(1, "gs0"))
+        gs_halves.append(quantise("gs1", score_gradient(1), HALF))
         gq_banks = []
         for h in range(2):
             gs_codes, gs_scales = gs_halves[h]
             bank = ps.tile([P, PACK, HALF], F32, name="gq%d" % h, tag="a%d" % h)
             for t in range(PACK):
-                cols = slice(P * t, P * (t + 1))
+                kt_codes, kt_scales = kt_pairs[t // 2]
+                cols = slice(P * (t % 2), P * (t % 2 + 1))
                 nc.tensor.matmul_mx(
                     out=bank[:, t, :],
                     lhsT=kt_codes[:, cols].bitcast(FP8X4),
@@ -283,7 +288,7 @@ def tile_attend_bteamshares_q_pl_kernel(
         y_halves = []
         for h in range(2):
             cols = slice(h * HALF, (h + 1) * HALF)
-            y = sbuf("y%d" % h, [P, PACK, HALF], F32, "gs%d" % (1 - h))
+            y = sbuf("y%d" % h, [P, PACK, HALF], F32, "gs1" if h == 0 else None)
             nc.vector.tensor_tensor(y[:], gq_banks[h][:], res_sb[:, :, cols], ALU.add)
             nc.sync.dma_start(y_rows[:, :, cols], y[:])
             y_halves.append(y)

@@ -66,9 +66,14 @@ def tile_attend_bteamshares_q_pl_kernel(
 
         keyrow_planes = keyrows.rearrange("(p t) c -> t p c", t=PACK)
 
+        def column_pieces(pieces):
+            return [slice(n * T // pieces, (n + 1) * T // pieces) for n in range(pieces)]
+
         def load_plane(t):
             plane = sbuf("plane%d" % t, [P, T], F32)
-            nc.sync.dma_start(plane[:], keyrow_planes[t])
+            pieces = 2 if t in SCALAR_PLANES else 1
+            for cols in column_pieces(pieces):
+                nc.sync.dma_start(plane[:, cols], keyrow_planes[t][:, cols])
             return plane
 
         keys_pool_words = load_words("keys_pool_words", keys_words)
@@ -184,7 +189,8 @@ def tile_attend_bteamshares_q_pl_kernel(
             listed = sbuf("kr_listed%d" % t, [P, I], BF16)
             if t in SCALAR_PLANES:
                 rounded = sbuf("kr_rounded%d" % t, [P, T], BF16)
-                nc.scalar.activation(rounded[:], planes[t][:], ACT.Copy)
+                for cols in column_pieces(2):
+                    nc.scalar.activation(rounded[:, cols], planes[t][:, cols], ACT.Copy)
                 nc.scalar.activation(listed[:], rounded[:].indirect(offsets[:]), ACT.Copy)
             else:
                 nc.vector.tensor_copy(listed[:], planes[t][:].indirect(offsets[:]))

from contextlib import ExitStack

import concourse.mybir as mybir
from concourse.masks import make_identity

D, E, T, I, Q, G = 512, 512, 2048, 512, 256, 32
FLOPS = 2 * I * Q * (D + E + D)

F32 = mybir.dt.float32
BF16 = mybir.dt.bfloat16
I32 = mybir.dt.int32
U32 = mybir.dt.uint32
U16 = mybir.dt.uint16
U8 = mybir.dt.uint8
FP8X4 = mybir.dt.float8_e4m3fn_x4
FP4X4 = mybir.dt.float4_e2m1fn_x4
ALU = mybir.AluOpType
ACT = mybir.ActivationFunctionType

P = 128
PACK = 4
TEAM = Q // G
HALF = Q // 2
GH = G // 2
SCALAR_PLANES = (1, 2)


def tile_attend_bteamshares_q_pl_kernel(
    tc, query, keys_words, keys_scales, reserve, us, gout, vals_words, vals_scales, fs, keyrows, res, offs,
    out_0, out_1, out_2,
):
    nc = tc.nc
    with ExitStack() as ctx:
        sb = ctx.enter_context(tc.tile_pool(name="sb", bufs=1))
        ps = ctx.enter_context(tc.psum_pool(name="ps", bufs=1))

        def sbuf(name, shape, dtype, tag=None):
            return sb.tile(shape, dtype, name=name, tag=tag or name, align_bytes=64)


        def load_scales(name, scales):
            pool_scales = sbuf(name, [P, T], U8)
            nc.vector.memset(pool_scales[:, : T // 2].bitcast(I32), 0)
            nc.gpsimd.memset(pool_scales[:, T // 2 :].bitcast(I32), 0)
            for quad in range(4):
                nc.sync.dma_start(
                    pool_scales[quad:P:32, :].bitcast(I32),
                    scales[0].rearrange("(b r) c -> r b c", r=4)[quad].bitcast(I32),
                )
            return pool_scales

        def load_words(name, words):
            pool_words = sbuf(name, [P, T], U16)
            nc.sync.dma_start(pool_words[:].bitcast(I32), words[0].bitcast(I32))
            return pool_words

        def load_rows(name, rows, tag=None):
            raw = sbuf(name, [P, PACK, Q], F32, tag)
            nc.sync.dma_start(raw[:], rows.rearrange("(p t) q -> p t q", t=PACK))
            return raw

        def load_slot_vector(name, vec):
            cols = sbuf(name, [P, PACK], F32)
            nc.sync.dma_start(cols[:], vec.rearrange("(p r) o -> p (r o)", r=PACK))
            return cols

        keyrow_planes = keyrows.rearrange("(p t) c -> t p c", t=PACK)

        def column_pieces(pieces):
            return [slice(n * T // pieces, (n + 1) * T // pieces) for n in range(pieces)]

        def load_plane(t):
            plane = sbuf("plane%d" % t, [P, T], F32)
            pieces = 2 if t in SCALAR_PLANES else 1
            for cols in column_pieces(pieces):
                nc.sync.dma_start(plane[:, cols], keyrow_planes[t][:, cols])
            return plane

        keys_pool_words = load_words("keys_pool_words", keys_words)
        offsets = sb.tile([P, I // 16], U16, name="offsets")
        nc.sync.dma_start(offsets[:], offs)
        query_raw = load_rows("query_raw", query)
        keys_pool_scales = load_scales("keys_pool_scales", keys_scales)
        vals_pool_words = load_words("vals_pool_words", vals_words)
        gout_raw = load_rows("gout_raw", gout)
        vals_pool_scales = load_scales("vals_pool_scales", vals_scales)
        reserve_cols = load_slot_vector("reserve_cols", reserve)
        planes = [load_plane(0)]
        us_cols = load_slot_vector("us_cols", us)
        fs_cols = load_slot_vector("fs_cols", fs)
        for t in range(1, PACK):
            planes.append(load_plane(t))
        res_sb = load_rows("res_sb", res)

        ident = sbuf("ident", [P, P], F32)
        make_identity(nc, ident[:])

        def gather(name, pool_tile, dtype):
            listed = sbuf(name + "_listed", [P, I], dtype)
            nc.vector.tensor_copy(listed[:], pool_tile[:].indirect(offsets[:]))
            return listed

        def deal_scales(name, listed, tag):
            dealt = sbuf(name + "_dealt", [P, I], U8, tag)
            nc.vector.tensor_copy(
                dealt[:].rearrange("p (r s) -> p r s", r=PACK),
                listed[:].rearrange("p (s r) -> p r s", r=PACK),
            )
            return dealt

        def deal_words(name, listed, tag):
            dealt = sbuf(name + "_dealt", [P, 2 * I], U8, tag)
            nc.vector.tensor_copy(
                dealt[:].bitcast(U16).rearrange("p (r s) -> p r s", r=PACK),
                listed[:].rearrange("p (s r) -> p r s", r=PACK),
            )
            return dealt

        def group_rows(name, raw):
            grouped = sbuf(name + "_grouped", [P, Q * PACK], BF16)
            nc.scalar.activation(
                grouped[:].rearrange("p (c i t) -> p c t i", i=4, t=PACK),
                raw[:].rearrange("p t (c i) -> p c t i", i=4),
                ACT.Copy,
            )
            return grouped

        def quantise(name, grouped, width, tag=None):
            codes = sbuf(name + "_codes", [P, width], U32, tag)
            scales = sbuf(name + "_scales", [P, width], U8)
            nc.vector.quantize_mx(out=codes[:].bitcast(FP8X4), scales=scales[:], in_=grouped[:])
            return codes, scales

        def slot_products(tag, words, word_scales, codes, scales):
            banks = []
            for h in range(2):
                bank = ps.tile([P, PACK, HALF], F32, name="%s%d" % (tag, h), tag="%s%d" % (tag, h))
                cols = slice(h * HALF, (h + 1) * HALF)
                for r in range(PACK):
                    nc.tensor.matmul_mx(
                        out=bank[:, r, :],
                        lhsT=words[:, 2 * P * r : 2 * P * (r + 1)].bitcast(FP4X4),
                        lhsT_scale=word_scales[:, P * r : P * (r + 1)],
                        rhs=codes[:, cols].bitcast(FP8X4),
                        rhs_scale=scales[:, cols],
                        start=True,
                        stop=True,
                    )
                banks.append(bank)
            return banks

        def by_member(bank):
            return bank[:].rearrange("p r (g j) -> p g j r", j=TEAM)

        def half_of(tile, h):
            return tile[:].rearrange("p j (g r) -> p g j r", r=PACK)[:, h * GH : (h + 1) * GH, :, :]

        keys_w_listed = gather("keys_w", keys_pool_words, U16)
        keys_s_listed = gather("keys_s", keys_pool_scales, U8)
        query_grouped = group_rows("query", query_raw)
        keys_w = deal_words("keys_w", keys_w_listed, "query_raw")
        query_codes, query_scales = quantise("query", query_grouped, Q)
        keys_s = deal_scales("keys_s", keys_s_listed, "keys_w_listed")
        vals_w_listed = gather("vals_w", vals_pool_words, U16)
        vals_s_listed = gather("vals_s", vals_pool_scales, U8)
        gout_grouped = group_rows("gout", gout_raw)
        vals_w = deal_words("vals_w", vals_w_listed, "vals_pool_scales")
        vals_s = deal_scales("vals_s", vals_s_listed, "vals_w_listed")

        a_banks = slot_products("a", keys_w, keys_s, query_codes, query_scales)

        p = sbuf("p", [P, TEAM, P], F32, "gout_raw")
        for h in range(2):
            nc.scalar.activation(half_of(p, h), by_member(a_banks[h]), ACT.Exp)

        reserve_wide = sbuf("reserve_wide", [P, G, PACK], F32)
        nc.scalar.copy(reserve_wide[:], reserve_cols[:].unsqueeze(1).to_broadcast([P, G, PACK]))
        sums = ps.tile([P, 2, P], F32, name="sums")
        members = [p[:, j, :] for j in range(TEAM)]
        terms = members[:1] + [reserve_wide[:].rearrange("p g r -> p (g r)")] + members[1:]
        for n, term in enumerate(terms):
            nc.tensor.matmul(
                sums[:, 0, :], lhsT=term, rhs=ident[:], is_transpose=True, start=(n == 0), stop=(n == TEAM)
            )
        gout_codes, gout_scales = quantise("gout", gout_grouped, Q, "reserve_wide")
        c_banks = slot_products("c", vals_w, vals_s, gout_codes, gout_scales)

        def gather_plane(t):
            listed = sbuf("kr_listed%d" % t, [P, I], BF16)
            if t in SCALAR_PLANES:
                rounded = sbuf("kr_rounded%d" % t, [P, T], BF16)
                for cols in column_pieces(2):
                    nc.scalar.activation(rounded[:, cols], planes[t][:, cols], ACT.Copy)
                nc.scalar.activation(listed[:], rounded[:].indirect(offsets[:]), ACT.Copy)
            else:
                nc.vector.tensor_copy(listed[:], planes[t][:].indirect(offsets[:]))
            return listed

        listed_planes = [gather_plane(0)]
        usfs = sbuf("usfs", [P, PACK], F32)
        nc.vector.tensor_tensor(usfs[:], us_cols[:], fs_cols[:], ALU.mult)
        inv_t = sbuf("inv_t", [P, P], F32, "us_cols")
        nc.vector.reciprocal(inv_t[:], sums[:, 0, :])
        nc.tensor.transpose(sums[:, 1, :], inv_t[:], ident[:])

        dsums = ps.tile([P, 2, P], F32, name="dsums")

        dbr = sbuf("dbr", [P, TEAM, P], F32, "fs_cols")
        for h in range(2):
            nc.vector.tensor_tensor(half_of(dbr, h), by_member(c_banks[h]), half_of(p, h), ALU.mult)
        for j in range(TEAM):
            nc.tensor.matmul(
                dsums[:, 0, :], lhsT=dbr[:, j, :], rhs=ident[:], is_transpose=True,
                start=(j == 0), stop=(j == TEAM - 1),
            )
        gain = sbuf("gain", [P, G, PACK], F32)
        nc.vector.tensor_tensor(
            gain[:],
            sums[:, 1, :].rearrange("p (g r) -> p g r", r=PACK),
            usfs[:].unsqueeze(1).to_broadcast([P, G, PACK]),
            ALU.mult,
        )
        share = sbuf("share", [P, TEAM, P], F32)
        nc.vector.tensor_tensor(
            share[:], p[:], gain[:].rearrange("p g r -> p (g r)").unsqueeze(1).to_broadcast([P, TEAM, P]), ALU.mult
        )
        mean_t = sbuf("mean_t", [P, P], F32)
        nc.vector.tensor_tensor(mean_t[:], dsums[:, 0, :], inv_t[:], ALU.mult)
        nc.tensor.transpose(dsums[:, 1, :], mean_t[:], ident[:])

        for t in range(1, PACK):
            listed_planes.append(gather_plane(t))
        mean = sbuf("mean", [P, G, PACK], F32, "plane%d" % (PACK - 1))
        nc.vector.tensor_copy(mean[:].rearrange("p g r -> p (g r)"), dsums[:, 1, :])
        kt_grouped = sbuf("kt_grouped", [P, D * PACK], BF16, "kr_rounded%d" % SCALAR_PLANES[-1])

        def turn_plane(t):
            pairs = listed_planes[t][:].bitcast(F32)
            turned = ps.tile([P, 2, P], F32, name="turned%d" % t, tag=("sums", "turned1", "turned2", "dsums")[t])
            for u in range(2):
                nc.tensor.transpose(turned[:, u, :], pairs[:, u : I // 2 : 2], ident[:])
            nc.scalar.copy(
                kt_grouped[:, P * PACK * t : P * PACK * (t + 1)].bitcast(F32).rearrange("p (m u) -> p m u", u=2),
                turned[:].rearrange("p u m -> p m u"),
            )

        for t in range(PACK):
            turn_plane(t)

        centred = sbuf("centred", [P, 2, GH, TEAM, PACK], F32)
        for h in range(2):
            nc.vector.tensor_tensor(
                centred[:, h],
                by_member(c_banks[h]),
                mean[:, h * GH : (h + 1) * GH, :].unsqueeze(2).to_broadcast([P, GH, TEAM, PACK]),
                ALU.subtract,
            )

        def score_gradient(h):
            gs = sbuf("gs%d" % h, [P, HALF * PACK], BF16)
            nc.vector.tensor_tensor(
                gs[:].rearrange("p (g j r) -> p g j r", j=TEAM, r=PACK), centred[:, h], half_of(share, h), ALU.mult
            )
            return gs

        def quantise_key_pair(pair, tag):
            width = 2 * P
            return quantise("kt%d" % pair, kt_grouped[:, pair * width * PACK : (pair + 1) * width * PACK], width, tag)

        gs_first = score_gradient(0)
        kt_pairs = [quantise_key_pair(0, "plane%d" % (PACK - 1))]
        gs_halves = [quantise("gs0", gs_first, HALF)]
        kt_pairs.append(quantise_key_pair(1, "gs0"))
        gs_halves.append(quantise("gs1", score_gradient(1), HALF))
        gq_banks = []
        for h in range(2):
            gs_codes, gs_scales = gs_halves[h]
            bank = ps.tile([P, PACK, HALF], F32, name="gq%d" % h, tag="a%d" % h)
            for t in range(PACK):
                kt_codes, kt_scales = kt_pairs[t // 2]
                cols = slice(P * (t % 2), P * (t % 2 + 1))
                nc.tensor.matmul_mx(
                    out=bank[:, t, :],
                    lhsT=kt_codes[:, cols].bitcast(FP8X4),
                    lhsT_scale=kt_scales[:, cols],
                    rhs=gs_codes[:].bitcast(FP8X4),
                    rhs_scale=gs_scales[:],
                    start=True,
                    stop=True,
                )
            gq_banks.append(bank)

        y_rows = out_0.rearrange("(p t) q -> p t q", t=PACK)
        y_halves = []
        for h in range(2):
            cols = slice(h * HALF, (h + 1) * HALF)
            y = sbuf("y%d" % h, [P, PACK, HALF], F32, "gs1" if h == 0 else None)
            nc.vector.tensor_tensor(y[:], gq_banks[h][:], res_sb[:, :, cols], ALU.add)
            nc.sync.dma_start(y_rows[:, :, cols], y[:])
            y_halves.append(y)
        y_grouped = sbuf("y_grouped", [P, Q * PACK], BF16)
        for h in range(2):
            dst = y_grouped[:, h * HALF * PACK : (h + 1) * HALF * PACK].rearrange("p (c i t) -> p c t i", i=4, t=PACK)
            src = y_halves[h][:].rearrange("p t (c i) -> p c t i", i=4)
            if h == 0:
                nc.scalar.copy(dst, src)
            else:
                nc.vector.tensor_copy(dst, src)
        y_codes, y_scales = quantise("y", y_grouped, Q)
        nc.sync.dma_start(out_1[0].rearrange("p c r -> p (c r)").bitcast(I32), y_codes[:].bitcast(I32))
        for quad in range(4):
            queue = nc.scalar if quad % 2 == 0 else nc.sync
            queue.dma_start(
                out_2[0].rearrange("(b r) c -> r b c", r=4)[quad].bitcast(I32),
                y_scales[quad:P:32, :].bitcast(I32),
            )
